import numpy as np
import ml_dtypes


def mxq(x, axis, fmt="e4m3"):
    dtype, down = {"e4m3": (ml_dtypes.float8_e4m3fn, 7), "e5m2": (ml_dtypes.float8_e5m2, 14)}[fmt]
    v = np.moveaxis(np.asarray(x, np.float32).astype(ml_dtypes.bfloat16).astype(np.float64), axis, -1)
    blocks = v.reshape(v.shape[:-1] + (-1, 32))
    amax = np.abs(blocks).max(-1, keepdims=True)
    byte = np.maximum(np.where(amax > 0, np.frexp(amax)[1] - 1 + 127, 0) - down, 1)
    scale = np.exp2(byte - 127.0)
    codes = (blocks / scale).astype(np.float32).astype(dtype).astype(np.float64)
    return np.moveaxis((codes * scale).reshape(v.shape), -1, axis)


WIDE = False


def mx_kscale(k, group=512):
    if not WIDE:
        return np.ones(k)
    levels = np.array([10, -10, 5, -5, 0])
    if group != 512:
        return np.exp2(np.random.permutation(np.resize(levels, k // group))).repeat(group)
    if k % 512:
        return np.exp2(np.random.permutation(np.resize(levels, k // 32))).repeat(32)
    a = np.empty((k // 512, 16))
    for p in range(k // 512):
        a[p, :8] = np.random.permutation(np.resize(levels, 8))
        for g in range(8):
            far = levels[np.abs(levels - a[p, g]) >= 10]
            a[p, g + 8] = far[np.random.randint(len(far))]
    return np.exp2(a.ravel()).repeat(32)


def f64(x):
    return np.asarray(x).astype(np.float64)


def striped(idx):
    return np.tile(np.asarray(idx).reshape(-1, 16).T, (8, 1)).astype(np.uint16)


def unstriped(offs):
    return offs[:16].T.reshape(-1).astype(np.int64)


H, KV, D, NQ, N = 8, 2, 128, 512, 512


def setup_inputs():
    n = np.random.standard_normal
    s = mx_kscale(D, 0)[:, None]
    u = mx_kscale(N)
    t = np.random.uniform(0.5, 2.0, N) * u
    v = n((KV, N, 128))
    return {
        "qT": (n((H, D, NQ)) * s * (0.70 / np.sqrt(D))).astype(np.float32),
        "kT": (n((KV, D, N)) / s).astype(np.float32),
        "t": t.reshape(N, 1).astype(np.float32),
        "v": (v / t[:, None]).astype(np.float32),
        "kb": (0.5 * n((N, 1))).astype(np.float32),
        "mask": (np.arange(N)[:, None] <= np.sort(np.random.randint(N // 4, N, NQ))[None, :]).astype(np.float32),
        "og": n((H, NQ, 128)).astype(np.float32),
    }


def reference(qT, kT, t, v, kb, mask, og):
    a = np.repeat(mxq(f64(kT), 1, "e4m3"), H // KV, 0).transpose(0, 2, 1) @ mxq(f64(qT), 1, "e4m3")
    a = a + f64(kb)
    p = np.tanh(a)
    p = p * f64(mask)
    w = p * f64(t)
    y = mxq(w, 1, "e4m3").transpose(0, 2, 1) @ np.repeat(mxq(f64(v), 1, "e4m3"), H // KV, 0)
    y = y / 16.0
    y = y / (1.0 + np.exp(-f64(og)))
    return y

@@ -1,0 +1,268 @@
+from contextlib import ExitStack
+
+import concourse.mybir as mybir
+
+H, KV, D, NQ, N = 8, 2, 128, 512, 512
+FLOPS = 2 * 2 * H * N * NQ * D
+
+F32 = mybir.dt.float32
+BF16 = mybir.dt.bfloat16
+U32 = mybir.dt.uint32
+U8 = mybir.dt.uint8
+FP8X4 = mybir.dt.float8_e4m3fn_x4
+ALU = mybir.AluOpType
+ACT = mybir.ActivationFunctionType
+
+P = 128
+PACK = 4
+ROWS = 32
+HALF = 256
+CH = 128
+SETS = ((2, 3, 4, 5), (0, 1, 6, 7))
+MUL_RUN = 2
+CAST_RUN = 4
+
+
+def tile_rows_a_tanh_kb_mask_gate_kernel(tc, qT, kT, t, v, kb, mask, og, out):
+    nc = tc.nc
+    with ExitStack() as ctx:
+        keep = ctx.enter_context(tc.tile_pool(name="keep", bufs=1))
+        work = ctx.enter_context(tc.tile_pool(name="work", bufs=3))
+        psum = ctx.enter_context(tc.psum_pool(name="psum", bufs=1))
+        ctx.enter_context(tc.manual_schedule())
+
+        def sb(name, shape, dt):
+            return keep.tile(shape, dt, name=name, align_bytes=64)
+
+        score_banks = [[psum.tile([P, 2, HALF], F32, name="sc%d_%d" % (g, b)) for b in range(2 - g % 2)] for g in range(4)]
+        y_banks = [psum.tile([P, 2, HALF], F32, name="y%d" % b) for b in range(2)]
+
+        k_raw = sb("k_raw", [P, PACK, N], F32)
+        kb_t = sb("kb_t", [P, PACK], F32)
+        t_t = sb("t_t", [P, PACK], F32)
+        q_raw = {(0, 0): sb("q_raw00", [P, PACK, HALF], F32), (0, 1): sb("q_raw01", [P, PACK, HALF], F32)}
+        q_raw1 = sb("q_raw1", [P, PACK, NQ], F32)
+        m_raw = [sb("m_raw%d" % u, [P, PACK, HALF], F32) for u in range(2)]
+        v_raw = sb("v_raw", [P, KV, PACK, D], F32)
+        gate = [sb("gate%d" % i, [P, 2, NQ // CH, D], F32) for i in range(4)]
+
+        def q_rows(h0, nh):
+            return qT[h0 : h0 + nh].rearrange("h (p j) n -> (h p) j n", j=PACK)
+
+        def load_og(i):
+            h0 = SETS[i // 2][2 * (i % 2)]
+            nc.sync.dma_start(out=gate[i][:].rearrange("p h m e -> p (h m) e"), in_=og[h0 : h0 + 2].rearrange("h (m p) e -> p (h m) e", p=P))
+
+        mask_rows = mask.rearrange("(p j) n -> p j n", j=PACK)
+        nc.sync.dma_start(out=q_raw[0, 0][:], in_=q_rows(2, 4)[:, :, 0:HALF])
+        for g in range(4):
+            eng = nc.sync if g < 2 else nc.scalar
+            eng.dma_start(out=k_raw[ROWS * g : ROWS * (g + 1)], in_=kT[g // 2].rearrange("(p j) n -> p j n", j=PACK))
+        nc.scalar.dma_start(out=kb_t[:], in_=kb.rearrange("(p j) o -> p (j o)", j=PACK))
+        nc.scalar.dma_start(out=t_t[:], in_=t.rearrange("(p j) o -> p (j o)", j=PACK))
+        nc.sync.dma_start(out=m_raw[0][:], in_=mask_rows[:, :, 0:HALF])
+        nc.sync.dma_start(out=v_raw[:].rearrange("p k j e -> p k (j e)"), in_=v.rearrange("k (p j) e -> p k (j e)", j=PACK))
+        nc.sync.dma_start(out=q_raw[0, 1][:], in_=q_rows(2, 4)[:, :, HALF:NQ])
+        nc.sync.dma_start(out=m_raw[1][:], in_=mask_rows[:, :, HALF:NQ])
+        load_og(0)
+        nc.sync.dma_start(out=q_raw1[0:64], in_=q_rows(0, 2))
+
+        def copy_on(eng, dst, src):
+            if eng == "v":
+                nc.vector.tensor_copy(out=dst, in_=src)
+            else:
+                nc.scalar.copy(out=dst, in_=src)
+
+        def quantize(codes, scales, vals):
+            nc.vector.quantize_mx(out=codes.bitcast(FP8X4), scales=scales, in_=vals)
+
+        q_bf, q_codes, q_scales = {}, {}, {}
+
+        def cast_q(s, c0, nchunk, eng):
+            w = nchunk * CH
+            key = (s, c0)
+            q_bf[key] = sb("q_bf%d_%d" % key, [P, w, PACK], BF16)
+            if s == 0:
+                src = q_raw[0, c0 // 2][:, :, (c0 % 2) * CH : (c0 % 2) * CH + w]
+            else:
+                src = q_raw1[:, :, c0 * CH : c0 * CH + w]
+            copy_on(eng, q_bf[key][:].rearrange("p (c i) j -> p c j i", i=CAST_RUN), src.rearrange("p j (c i) -> p c j i", i=CAST_RUN))
+
+        def quant_q(s, c0, nchunk):
+            w = nchunk * CH
+            key = (s, c0)
+            codes = sb("q_codes%d_%d" % key, [P, w], U32)
+            scales = sb("q_scales%d_%d" % key, [P, w], U8)
+            quantize(codes[:], scales[:], q_bf[key][:].rearrange("p n j -> p (n j)"))
+            for c in range(nchunk):
+                q_codes[s, c0 + c] = codes[:, c * CH : (c + 1) * CH]
+                q_scales[s, c0 + c] = scales[:, c * CH : (c + 1) * CH]
+
+        k_bf = [sb("k_bf%d" % rp, [P, 2, CH, PACK], BF16) for rp in range(2)]
+        k_codes = [sb("k_codes%d" % rp, [P, 2 * CH], U32) for rp in range(2)]
+        k_scales = [sb("k_scales%d" % rp, [P, 2 * CH], U8) for rp in range(2)]
+
+        def cast_k(rp, eng):
+            src = k_raw[:].rearrange("p j (s r) -> p s j r", r=PACK)[:, :, :, 2 * rp : 2 * rp + 2]
+            copy_on(eng, k_bf[rp][:].rearrange("p r s j -> p s j r"), src)
+
+        def quant_k(rp):
+            quantize(k_codes[rp][:], k_scales[rp][:], k_bf[rp][:].rearrange("p r s j -> p (r s j)"))
+
+        v_bf = sb("v_bf", [P, KV, D, PACK], BF16)
+        v_codes = sb("v_codes", [P, KV * D], U32)
+        v_scales = sb("v_scales", [P, KV * D], U8)
+
+        def cast_v(eng):
+            copy_on(eng, v_bf[:].rearrange("p k (c i) j -> p k c j i", i=CAST_RUN), v_raw[:].rearrange("p k j (c i) -> p k c j i", i=CAST_RUN))
+
+        def quant_v():
+            quantize(v_codes[:], v_scales[:], v_bf[:].rearrange("p k e j -> p (k e j)"))
+
+        mt = [sb("mt%d" % u, [P, PACK, HALF], F32) for u in range(2)]
+
+        def make_mt(u):
+            for r in range(PACK):
+                nc.vector.tensor_scalar(out=mt[u][:, r, :], in0=m_raw[u][:, r, :], scalar1=t_t[:, r : r + 1], scalar2=1.0 / 32.0, op0=ALU.mult, op1=ALU.mult)
+
+        steps = [(s, u, pr) for s in range(2) for u in range(2) for pr in range(2)]
+        n_steps = len(steps)
+        p_t = {}
+
+        def scores(k, e, rp):
+            s, u, pr = steps[k]
+            g = 2 * pr + e
+            if rp == 0:
+                p_t[k, e] = sb("p%d_%d" % (k, e), [P, PACK, HALF], F32)
+            bank = score_banks[g][rp % len(score_banks[g])]
+            rows = slice(ROWS * g, ROWS * (g + 1))
+            for r in range(2):
+                for c in range(2):
+                    nc.tensor.matmul_mx(
+                        out=bank[:, r, c * CH : (c + 1) * CH],
+                        lhsT=k_codes[rp][rows, r * CH : (r + 1) * CH].bitcast(FP8X4),
+                        lhsT_scale=k_scales[rp][rows, r * CH : (r + 1) * CH],
+                        rhs=q_codes[s, 2 * u + c][rows].bitcast(FP8X4),
+                        rhs_scale=q_scales[s, 2 * u + c][rows],
+                        start=True,
+                        stop=True,
+                    )
+            for r in range(2):
+                nc.scalar.activation(out=p_t[k, e][:, 2 * rp + r, :], in_=bank[:, r, :], func=ACT.Tanh, bias=kb_t[:, 2 * rp + r : 2 * rp + r + 1])
+
+        def gate_view(k):
+            s, u, pr = steps[k]
+            return gate[2 * s + pr][:, :, 2 * u : 2 * u + 2, :].rearrange("p h m e -> p h (m e)")
+
+        def gate_tanh(k):
+            nc.scalar.activation(out=gate_view(k), in_=gate_view(k), func=ACT.Tanh, scale=0.5)
+
+        w_bf, w_codes, w_scales = {}, {}, {}
+
+        def weigh(k, e):
+            u = steps[k][1]
+            w_bf[k, e] = work.tile([P, HALF, PACK], BF16, name="w_bf", align_bytes=64)
+            nc.vector.tensor_tensor(
+                out=w_bf[k, e][:].rearrange("p (c i) r -> p c r i", i=MUL_RUN),
+                in0=p_t[k, e][:].rearrange("p r (c i) -> p c r i", i=MUL_RUN),
+                in1=mt[u][:].rearrange("p r (c i) -> p c r i", i=MUL_RUN),
+                op=ALU.mult,
+            )
+
+        def quant_w(k, e):
+            w_codes[k, e] = work.tile([P, HALF], U32, name="w_codes", align_bytes=64)
+            w_scales[k, e] = work.tile([P, HALF], U8, name="w_scales", align_bytes=64)
+            quantize(w_codes[k, e][:], w_scales[k, e][:], w_bf[k, e][:].rearrange("p n r -> p (n r)"))
+
+        def y_bank(k, e):
+            return y_banks[(k + (1 if (k == n_steps - 1 and e == 1) else 0)) % 2]
+
+        def values(k, e):
+            pr = steps[k][2]
+            for c in range(2):
+                nc.tensor.matmul_mx(
+                    out=y_bank(k, e)[:, e, c * CH : (c + 1) * CH],
+                    lhsT=w_codes[k, e][:, c * CH : (c + 1) * CH].bitcast(FP8X4),
+                    lhsT_scale=w_scales[k, e][:, c * CH : (c + 1) * CH],
+                    rhs=v_codes[:, pr * D : (pr + 1) * D].bitcast(FP8X4),
+                    rhs_scale=v_scales[:, pr * D : (pr + 1) * D],
+                    start=True,
+                    stop=True,
+                )
+
+        def finish(k, es):
+            s, u, pr = steps[k]
+            res = sb("res%d_%d" % (k, es[0]), [P, len(es), HALF], F32)
+            lo, hi = es[0], es[-1] + 1
+            nc.vector.scalar_tensor_tensor(out=res[:], in0=gate_view(k)[:, lo:hi, :], scalar=1.0, in1=y_bank(k, es[0])[:, lo:hi, :], op0=ALU.add, op1=ALU.mult)
+            for n, e in enumerate(es):
+                h = SETS[s][2 * pr + e]
+                nc.sync.dma_start(out=out[h, u * HALF : (u + 1) * HALF, :].rearrange("(m p) e -> p m e", p=P), in_=res[:, n, :].rearrange("p (m e) -> p m e", e=D))
+
+        def score_step(k):
+            if k == 0:
+                scores(0, 0, 0)
+                scores(0, 0, 1)
+                scores(0, 1, 0)
+                scores(0, 1, 1)
+                return
+            scores(k, 1, 0)
+            scores(k, 0, 0)
+            scores(k, 0, 1)
+            if k >= 2:
+                gate_tanh(k - 2)
+            scores(k, 1, 1)
+
+        cast_q(0, 0, 1, "v")
+        cast_q(0, 1, 1, "v")
+        quant_q(0, 0, 1)
+        quant_q(0, 1, 1)
+        cast_k(0, "v")
+        cast_k(1, "s")
+        quant_k(0)
+        quant_k(1)
+        score_step(0)
+        make_mt(0)
+        cast_v("v")
+
+        for k in range(n_steps):
+            if k == 2:
+                cast_q(1, 0, 2, "s")
+            if k == 4:
+                cast_q(1, 2, 2, "s")
+            if k + 1 < n_steps:
+                score_step(k + 1)
+            else:
+                gate_tanh(k - 1)
+                gate_tanh(k)
+            if k == 0:
+                nc.scalar.dma_start(out=q_raw1[64:128], in_=q_rows(6, 2))
+                load_og(1)
+                load_og(2)
+                load_og(3)
+            weigh(k, 0)
+            if k == 0:
+                quant_v()
+                cast_q(0, 2, 2, "v")
+            else:
+                quant_w(k - 1, 1)
+                values(k - 1, 0)
+                values(k - 1, 1)
+            weigh(k, 1)
+            if k == 0:
+                quant_q(0, 2, 2)
+            if k == 2:
+                quant_q(1, 0, 2)
+            if k == 4:
+                quant_q(1, 2, 2)
+            quant_w(k, 0)
+            if k == 1:
+                make_mt(1)
+            if k > 0:
+                finish(k - 1, [0, 1])
+        last = n_steps - 1
+        values(last, 0)
+        quant_w(last, 1)
+        values(last, 1)
+        finish(last, [0])
+        finish(last, [1])

@@ -19,7 +19,7 @@ ROWS = 32
 HALF = 256
 CH = 128
 SETS = ((2, 3, 4, 5), (0, 1, 6, 7))
-MUL_RUN = 2
+MUL_RUN = 4
 CAST_RUN = 4
 
 
@@ -27,15 +27,15 @@ def tile_rows_a_tanh_kb_mask_gate_kernel(tc, qT, kT, t, v, kb, mask, og, out):
     nc = tc.nc
     with ExitStack() as ctx:
         keep = ctx.enter_context(tc.tile_pool(name="keep", bufs=1))
-        work = ctx.enter_context(tc.tile_pool(name="work", bufs=3))
+        work = ctx.enter_context(tc.tile_pool(name="work", bufs=6))
         psum = ctx.enter_context(tc.psum_pool(name="psum", bufs=1))
         ctx.enter_context(tc.manual_schedule())
 
         def sb(name, shape, dt):
             return keep.tile(shape, dt, name=name, align_bytes=64)
 
-        score_banks = [[psum.tile([P, 2, HALF], F32, name="sc%d_%d" % (g, b)) for b in range(2 - g % 2)] for g in range(4)]
-        y_banks = [psum.tile([P, 2, HALF], F32, name="y%d" % b) for b in range(2)]
+        score_banks = [[psum.tile([P, NQ], F32, name="sc%d_%d" % (g, b)) for b in range(2 - g // 3)] for g in range(4)]
+        y_bank = psum.tile([P, NQ], F32, name="y_bank")
 
         k_raw = sb("k_raw", [P, PACK, N], F32)
         kb_t = sb("kb_t", [P, PACK], F32)
@@ -54,17 +54,16 @@ def tile_rows_a_tanh_kb_mask_gate_kernel(tc, qT, kT, t, v, kb, mask, og, out):
             nc.sync.dma_start(out=gate[i][:].rearrange("p h m e -> p (h m) e"), in_=og[h0 : h0 + 2].rearrange("h (m p) e -> p (h m) e", p=P))
 
         mask_rows = mask.rearrange("(p j) n -> p j n", j=PACK)
-        nc.sync.dma_start(out=q_raw[0, 0][:], in_=q_rows(2, 4)[:, :, 0:HALF])
         for g in range(4):
             eng = nc.sync if g < 2 else nc.scalar
             eng.dma_start(out=k_raw[ROWS * g : ROWS * (g + 1)], in_=kT[g // 2].rearrange("(p j) n -> p j n", j=PACK))
+        nc.sync.dma_start(out=q_raw[0, 0][:], in_=q_rows(2, 4)[:, :, 0:HALF])
         nc.scalar.dma_start(out=kb_t[:], in_=kb.rearrange("(p j) o -> p (j o)", j=PACK))
         nc.scalar.dma_start(out=t_t[:], in_=t.rearrange("(p j) o -> p (j o)", j=PACK))
         nc.sync.dma_start(out=m_raw[0][:], in_=mask_rows[:, :, 0:HALF])
-        nc.sync.dma_start(out=v_raw[:].rearrange("p k j e -> p k (j e)"), in_=v.rearrange("k (p j) e -> p k (j e)", j=PACK))
         nc.sync.dma_start(out=q_raw[0, 1][:], in_=q_rows(2, 4)[:, :, HALF:NQ])
+        nc.sync.dma_start(out=v_raw[:].rearrange("p k j e -> p k (j e)"), in_=v.rearrange("k (p j) e -> p k (j e)", j=PACK))
         nc.sync.dma_start(out=m_raw[1][:], in_=mask_rows[:, :, HALF:NQ])
-        load_og(0)
         nc.sync.dma_start(out=q_raw1[0:64], in_=q_rows(0, 2))
 
         def copy_on(eng, dst, src):
@@ -119,150 +118,177 @@ def tile_rows_a_tanh_kb_mask_gate_kernel(tc, qT, kT, t, v, kb, mask, og, out):
         def quant_v():
             quantize(v_codes[:], v_scales[:], v_bf[:].rearrange("p k e j -> p (k e j)"))
 
-        mt = [sb("mt%d" % u, [P, PACK, HALF], F32) for u in range(2)]
+        mt = sb("mt", [P, NQ * PACK], F32)
 
         def make_mt(u):
+            half = mt[:, u * HALF * PACK : (u + 1) * HALF * PACK].rearrange("p (c r i) -> p c r i", r=PACK, i=MUL_RUN)
             for r in range(PACK):
-                nc.vector.tensor_scalar(out=mt[u][:, r, :], in0=m_raw[u][:, r, :], scalar1=t_t[:, r : r + 1], scalar2=1.0 / 32.0, op0=ALU.mult, op1=ALU.mult)
+                nc.vector.tensor_scalar(out=half[:, :, r, :], in0=m_raw[u][:, r, :].rearrange("p (c i) -> p c i", i=MUL_RUN), scalar1=t_t[:, r : r + 1], scalar2=1.0 / 32.0, op0=ALU.mult, op1=ALU.mult)
 
-        steps = [(s, u, pr) for s in range(2) for u in range(2) for pr in range(2)]
-        n_steps = len(steps)
-        p_t = {}
+        def half_item(g, u, rp):
+            return (0, g, (2 * rp, 2 * rp + 1), 2 * u, 2)
 
-        def scores(k, e, rp):
-            s, u, pr = steps[k]
-            g = 2 * pr + e
-            if rp == 0:
-                p_t[k, e] = sb("p%d_%d" % (k, e), [P, PACK, HALF], F32)
-            bank = score_banks[g][rp % len(score_banks[g])]
-            rows = slice(ROWS * g, ROWS * (g + 1))
-            for r in range(2):
-                for c in range(2):
+        def full_item(s, g, r):
+            return (s, g, (r,), 0, 4)
+
+        def bank_of(item):
+            s, g, rs, c0, nch = item
+            banks = score_banks[g]
+            return banks[(rs[0] // len(rs)) % len(banks)]
+
+        def fill(*items):
+            calls = [[(item, n, r, c) for c in range(item[4]) for n, r in enumerate(item[2])] for item in items]
+            for group in zip(*calls):
+                for item, n, r, c in group:
+                    s, g, rs, c0, nch = item
+                    rows = slice(ROWS * g, ROWS * (g + 1))
+                    col = (n * nch + c) * CH
+                    kc = slice((r % 2) * CH, (r % 2 + 1) * CH)
                     nc.tensor.matmul_mx(
-                        out=bank[:, r, c * CH : (c + 1) * CH],
-                        lhsT=k_codes[rp][rows, r * CH : (r + 1) * CH].bitcast(FP8X4),
-                        lhsT_scale=k_scales[rp][rows, r * CH : (r + 1) * CH],
-                        rhs=q_codes[s, 2 * u + c][rows].bitcast(FP8X4),
-                        rhs_scale=q_scales[s, 2 * u + c][rows],
+                        out=bank_of(item)[:, col : col + CH],
+                        lhsT=k_codes[r // 2][rows, kc].bitcast(FP8X4),
+                        lhsT_scale=k_scales[r // 2][rows, kc],
+                        rhs=q_codes[s, c0 + c][rows].bitcast(FP8X4),
+                        rhs_scale=q_scales[s, c0 + c][rows],
                         start=True,
                         stop=True,
                     )
-            for r in range(2):
-                nc.scalar.activation(out=p_t[k, e][:, 2 * rp + r, :], in_=bank[:, r, :], func=ACT.Tanh, bias=kb_t[:, 2 * rp + r : 2 * rp + r + 1])
 
-        def gate_view(k):
-            s, u, pr = steps[k]
-            return gate[2 * s + pr][:, :, 2 * u : 2 * u + 2, :].rearrange("p h m e -> p h (m e)")
+        p_t = {}
 
-        def gate_tanh(k):
-            nc.scalar.activation(out=gate_view(k), in_=gate_view(k), func=ACT.Tanh, scale=0.5)
+        def tanh(item):
+            s, g, rs, c0, nch = item
+            w = nch * CH
+            key = (s, g, c0)
+            if rs[0] == 0:
+                p_t[key] = sb("p%d_%d_%d" % key, [P, PACK, w], F32)
+            for n, r in enumerate(rs):
+                nc.scalar.activation(out=p_t[key][:, r, :], in_=bank_of(item)[:, n * w : (n + 1) * w], func=ACT.Tanh, bias=kb_t[:, r : r + 1])
+
+        def gate_view(s, g):
+            return gate[2 * s + g // 2][:, g % 2].rearrange("p m e -> p (m e)")
+
+        def gate_tanh(s, g):
+            nc.scalar.activation(out=gate_view(s, g), in_=gate_view(s, g), func=ACT.Tanh, scale=0.5)
 
         w_bf, w_codes, w_scales = {}, {}, {}
 
-        def weigh(k, e):
-            u = steps[k][1]
-            w_bf[k, e] = work.tile([P, HALF, PACK], BF16, name="w_bf", align_bytes=64)
+        def weigh(s, g, c0, nch):
+            w = nch * CH
+            w_bf[s, g, c0] = work.tile([P, w, PACK], BF16, name="w_bf", align_bytes=64)
+            if (s, g, c0) in p_t:
+                src = p_t[s, g, c0][:, :, 0:w]
+            else:
+                src = p_t[s, g, 0][:, :, c0 * CH : c0 * CH + w]
             nc.vector.tensor_tensor(
-                out=w_bf[k, e][:].rearrange("p (c i) r -> p c r i", i=MUL_RUN),
-                in0=p_t[k, e][:].rearrange("p r (c i) -> p c r i", i=MUL_RUN),
-                in1=mt[u][:].rearrange("p r (c i) -> p c r i", i=MUL_RUN),
+                out=w_bf[s, g, c0][:].rearrange("p (c i) r -> p c r i", i=MUL_RUN),
+                in0=src.rearrange("p r (c i) -> p c r i", i=MUL_RUN),
+                in1=mt[:, c0 * CH * PACK : (c0 * CH + w) * PACK].rearrange("p (c r i) -> p c r i", r=PACK, i=MUL_RUN),
                 op=ALU.mult,
             )
 
-        def quant_w(k, e):
-            w_codes[k, e] = work.tile([P, HALF], U32, name="w_codes", align_bytes=64)
-            w_scales[k, e] = work.tile([P, HALF], U8, name="w_scales", align_bytes=64)
-            quantize(w_codes[k, e][:], w_scales[k, e][:], w_bf[k, e][:].rearrange("p n r -> p (n r)"))
+        def quant_w(s, g, c0, nch):
+            w = nch * CH
+            codes = work.tile([P, w], U32, name="w_codes", align_bytes=64)
+            scales = work.tile([P, w], U8, name="w_scales", align_bytes=64)
+            quantize(codes[:], scales[:], w_bf[s, g, c0][:].rearrange("p n r -> p (n r)"))
+            for c in range(nch):
+                w_codes[s, g, c0 + c] = codes[:, c * CH : (c + 1) * CH]
+                w_scales[s, g, c0 + c] = scales[:, c * CH : (c + 1) * CH]
 
-        def y_bank(k, e):
-            return y_banks[(k + (1 if (k == n_steps - 1 and e == 1) else 0)) % 2]
-
-        def values(k, e):
-            pr = steps[k][2]
-            for c in range(2):
+        def values(s, g, c0=0, nch=4):
+            kv = g // 2
+            for c in range(c0, c0 + nch):
                 nc.tensor.matmul_mx(
-                    out=y_bank(k, e)[:, e, c * CH : (c + 1) * CH],
-                    lhsT=w_codes[k, e][:, c * CH : (c + 1) * CH].bitcast(FP8X4),
-                    lhsT_scale=w_scales[k, e][:, c * CH : (c + 1) * CH],
-                    rhs=v_codes[:, pr * D : (pr + 1) * D].bitcast(FP8X4),
-                    rhs_scale=v_scales[:, pr * D : (pr + 1) * D],
+                    out=y_bank[:, c * CH : (c + 1) * CH],
+                    lhsT=w_codes[s, g, c].bitcast(FP8X4),
+                    lhsT_scale=w_scales[s, g, c],
+                    rhs=v_codes[:, kv * D : (kv + 1) * D].bitcast(FP8X4),
+                    rhs_scale=v_scales[:, kv * D : (kv + 1) * D],
                     start=True,
                     stop=True,
                 )
 
-        def finish(k, es):
-            s, u, pr = steps[k]
-            res = sb("res%d_%d" % (k, es[0]), [P, len(es), HALF], F32)
-            lo, hi = es[0], es[-1] + 1
-            nc.vector.scalar_tensor_tensor(out=res[:], in0=gate_view(k)[:, lo:hi, :], scalar=1.0, in1=y_bank(k, es[0])[:, lo:hi, :], op0=ALU.add, op1=ALU.mult)
-            for n, e in enumerate(es):
-                h = SETS[s][2 * pr + e]
-                nc.sync.dma_start(out=out[h, u * HALF : (u + 1) * HALF, :].rearrange("(m p) e -> p m e", p=P), in_=res[:, n, :].rearrange("p (m e) -> p m e", e=D))
+        def finish(s, g, parts=1):
+            w = NQ // parts
+            for u in range(parts):
+                res = sb("res%d_%d_%d" % (s, g, u), [P, w], F32)
+                cols = slice(u * w, (u + 1) * w)
+                nc.vector.scalar_tensor_tensor(out=res[:], in0=gate_view(s, g)[:, cols], scalar=1.0, in1=y_bank[:, cols], op0=ALU.add, op1=ALU.mult)
+                (nc.sync, nc.scalar)[u].dma_start(out=out[SETS[s][g], cols, :].rearrange("(m p) e -> p m e", p=P), in_=res[:].rearrange("p (m e) -> p m e", e=D))
 
-        def score_step(k):
-            if k == 0:
-                scores(0, 0, 0)
-                scores(0, 0, 1)
-                scores(0, 1, 0)
-                scores(0, 1, 1)
-                return
-            scores(k, 1, 0)
-            scores(k, 0, 0)
-            scores(k, 0, 1)
-            if k >= 2:
-                gate_tanh(k - 2)
-            scores(k, 1, 1)
+        A, B, C, E = 0, 1, 2, 3
+        items = [half_item(A, 0, 0), half_item(A, 0, 1), half_item(B, 0, 0), half_item(B, 0, 1), half_item(A, 1, 0), half_item(A, 1, 1)]
+        items.extend([half_item(B, 1, 0), full_item(0, C, 0), half_item(B, 1, 1), full_item(0, C, 1)])
+        items.extend([full_item(0, E, 0), full_item(0, C, 2), full_item(0, E, 1), full_item(0, C, 3)])
+        items.extend([full_item(0, E, 2), full_item(1, A, 0), full_item(0, E, 3), full_item(1, A, 1)])
+        items.extend([full_item(1, B, 0), full_item(1, A, 2), full_item(1, B, 1), full_item(1, A, 3)])
+        items.extend([full_item(1, E, 0), full_item(1, B, 2), full_item(1, E, 1), full_item(1, B, 3)])
+        items.extend([full_item(1, E, 2), full_item(1, C, 0), full_item(1, E, 3), full_item(1, C, 1)])
+        items.extend([full_item(1, C, 2), full_item(1, C, 3)])
+        fills_after = {1: [(4, 7)], 2: [(5, 6)], 3: [(8, 9)], 7: [(10, 11)], 10: [(12, 13)], 12: [(14, 15)], 14: [(16, 17)], 15: [(18, 19)], 17: [(20, 21)], 18: [(22, 23)], 22: [(24, 25)], 24: [(26, 27)], 26: [(28, 29)], 27: [(30,)], 29: [(31,)]}
+        gate_after = {11: (0, A), 13: (0, B), 15: (0, C), 21: (0, E), 23: (1, A), 25: (1, B), 27: (1, E), 30: (1, C)}
+        heads = [(0, A), (0, B), (0, C), (0, E), (1, A), (1, B), (1, E), (1, C)]
+        done_at = {13: 2, 16: 3, 21: 4, 25: 5, 28: 6, 31: 7}
 
-        cast_q(0, 0, 1, "v")
-        cast_q(0, 1, 1, "v")
-        quant_q(0, 0, 1)
-        quant_q(0, 1, 1)
         cast_k(0, "v")
         cast_k(1, "s")
         quant_k(0)
+        cast_q(0, 0, 1, "v")
+        cast_q(0, 1, 1, "s")
         quant_k(1)
-        score_step(0)
+        quant_q(0, 0, 1)
+        quant_q(0, 1, 1)
+        fill(items[0], items[2])
+        fill(items[1], items[3])
         make_mt(0)
-        cast_v("v")
-
-        for k in range(n_steps):
-            if k == 2:
-                cast_q(1, 0, 2, "s")
-            if k == 4:
-                cast_q(1, 2, 2, "s")
-            if k + 1 < n_steps:
-                score_step(k + 1)
-            else:
-                gate_tanh(k - 1)
-                gate_tanh(k)
-            if k == 0:
-                nc.scalar.dma_start(out=q_raw1[64:128], in_=q_rows(6, 2))
-                load_og(1)
-                load_og(2)
-                load_og(3)
-            weigh(k, 0)
-            if k == 0:
-                quant_v()
-                cast_q(0, 2, 2, "v")
-            else:
-                quant_w(k - 1, 1)
-                values(k - 1, 0)
-                values(k - 1, 1)
-            weigh(k, 1)
-            if k == 0:
+        cast_q(0, 2, 2, "v")
+        for j, item in enumerate(items):
+            tanh(item)
+            if j == 1:
+                weigh(0, A, 0, 2)
                 quant_q(0, 2, 2)
-            if k == 2:
-                quant_q(1, 0, 2)
-            if k == 4:
-                quant_q(1, 2, 2)
-            quant_w(k, 0)
-            if k == 1:
+            if j == 2:
+                nc.scalar.dma_start(out=q_raw1[64:128], in_=q_rows(6, 2))
+                for i in range(4):
+                    load_og(i)
+            if j == 3:
+                cast_v("s")
+                weigh(0, B, 0, 2)
+                quant_w(0, A, 0, 2)
                 make_mt(1)
-            if k > 0:
-                finish(k - 1, [0, 1])
-        last = n_steps - 1
-        values(last, 0)
-        quant_w(last, 1)
-        values(last, 1)
-        finish(last, [0])
-        finish(last, [1])
+                quant_w(0, B, 0, 2)
+            if j == 5:
+                weigh(0, A, 2, 2)
+                quant_v()
+                quant_w(0, A, 2, 2)
+                cast_q(1, 0, 4, "v")
+            if j == 8:
+                weigh(0, B, 2, 2)
+                quant_q(1, 0, 4)
+                quant_w(0, B, 2, 2)
+            for group in fills_after.get(j, []):
+                fill(*[items[n] for n in group])
+            if j == 10:
+                values(0, A)
+            if j in gate_after:
+                gate_tanh(*gate_after[j])
+            if j == 11:
+                finish(0, A)
+            if j in done_at:
+                n = done_at[j]
+                s, g = heads[n]
+                values(*heads[n - 1])
+                if n < 7:
+                    weigh(s, g, 0, 4)
+                    finish(*heads[n - 1])
+                    quant_w(s, g, 0, 4)
+                else:
+                    weigh(s, g, 0, 2)
+                    weigh(s, g, 2, 2)
+                    quant_w(s, g, 0, 2)
+                    finish(*heads[n - 1])
+                    values(s, g, 0, 2)
+                    quant_w(s, g, 2, 2)
+                    values(s, g, 2, 2)
+                    finish(s, g, 2)

@@ -7,6 +7,7 @@ FLOPS = 2 * 2 * H * N * NQ * D
 
 F32 = mybir.dt.float32
 BF16 = mybir.dt.bfloat16
+I32 = mybir.dt.int32
 U32 = mybir.dt.uint32
 U8 = mybir.dt.uint8
 FP8X4 = mybir.dt.float8_e4m3fn_x4
@@ -16,279 +17,299 @@ ACT = mybir.ActivationFunctionType
 P = 128
 PACK = 4
 ROWS = 32
-HALF = 256
 CH = 128
+HALF = 256
+RUN = 4
 SETS = ((2, 3, 4, 5), (0, 1, 6, 7))
-MUL_RUN = 4
-CAST_RUN = 4
+A, B, C, E = 0, 2, 1, 3
+LOOKAHEAD = 4
+W_BUFS = 5
 
 
 def tile_rows_a_tanh_kb_mask_gate_kernel(tc, qT, kT, t, v, kb, mask, og, out):
     nc = tc.nc
     with ExitStack() as ctx:
         keep = ctx.enter_context(tc.tile_pool(name="keep", bufs=1))
-        work = ctx.enter_context(tc.tile_pool(name="work", bufs=6))
+        work = ctx.enter_context(tc.tile_pool(name="work", bufs=W_BUFS))
         psum = ctx.enter_context(tc.psum_pool(name="psum", bufs=1))
         ctx.enter_context(tc.manual_schedule())
 
-        def sb(name, shape, dt):
-            return keep.tile(shape, dt, name=name, align_bytes=64)
+        def sb(name, shape, dtype):
+            return keep.tile(shape, dtype, name=name, align_bytes=64)
 
-        score_banks = [[psum.tile([P, NQ], F32, name="sc%d_%d" % (g, b)) for b in range(2 - g // 3)] for g in range(4)]
+        def copy_on(engine, dst, src):
+            if engine is nc.vector:
+                nc.vector.tensor_copy(out=dst, in_=src)
+            else:
+                nc.scalar.copy(out=dst, in_=src)
+
+        def quantize(codes, scales, values):
+            nc.vector.quantize_mx(out=codes.bitcast(FP8X4), scales=scales, in_=values)
+
+        def multiply(dst, lhs_codes, lhs_scales, rhs_codes, rhs_scales):
+            nc.tensor.matmul_mx(
+                out=dst,
+                lhsT=lhs_codes.bitcast(FP8X4),
+                lhsT_scale=lhs_scales,
+                rhs=rhs_codes.bitcast(FP8X4),
+                rhs_scale=rhs_scales,
+                start=True,
+                stop=True,
+            )
+
+        score_banks = [[psum.tile([P, NQ], F32, name="scores%d_%d" % (g, b)) for b in range(1 if g == E else 2)] for g in range(4)]
         y_bank = psum.tile([P, NQ], F32, name="y_bank")
 
         k_raw = sb("k_raw", [P, PACK, N], F32)
         kb_t = sb("kb_t", [P, PACK], F32)
         t_t = sb("t_t", [P, PACK], F32)
-        q_raw = {(0, 0): sb("q_raw00", [P, PACK, HALF], F32), (0, 1): sb("q_raw01", [P, PACK, HALF], F32)}
-        q_raw1 = sb("q_raw1", [P, PACK, NQ], F32)
+        q_first = [sb("q_first%d" % u, [P, PACK, HALF], F32) for u in range(2)]
+        q_second = sb("q_second", [P, PACK, NQ], F32)
         m_raw = [sb("m_raw%d" % u, [P, PACK, HALF], F32) for u in range(2)]
         v_raw = sb("v_raw", [P, KV, PACK, D], F32)
-        gate = [sb("gate%d" % i, [P, 2, NQ // CH, D], F32) for i in range(4)]
+        gate = [sb("gate%d" % n, [P, 2, NQ], F32) for n in range(H // 2)]
 
-        def q_rows(h0, nh):
-            return qT[h0 : h0 + nh].rearrange("h (p j) n -> (h p) j n", j=PACK)
+        def q_rows(h0, heads):
+            return qT[h0 : h0 + heads].rearrange("h (p j) n -> (h p) j n", j=PACK)
 
-        def load_og(i):
-            h0 = SETS[i // 2][2 * (i % 2)]
-            nc.sync.dma_start(out=gate[i][:].rearrange("p h m e -> p (h m) e"), in_=og[h0 : h0 + 2].rearrange("h (m p) e -> p (h m) e", p=P))
+        def load_og(n):
+            h0 = SETS[n // 2][2 * (n % 2)]
+            rows = og[h0 : h0 + 2].rearrange("h (u a x) e -> a (h u) (x e)", u=2, x=2)
+            nc.sync.dma_start(out=gate[n][:].rearrange("p h (u c) -> p (h u) c", u=2), in_=rows)
 
-        mask_rows = mask.rearrange("(p j) n -> p j n", j=PACK)
-        for g in range(4):
-            eng = nc.sync if g < 2 else nc.scalar
-            eng.dma_start(out=k_raw[ROWS * g : ROWS * (g + 1)], in_=kT[g // 2].rearrange("(p j) n -> p j n", j=PACK))
-        nc.sync.dma_start(out=q_raw[0, 0][:], in_=q_rows(2, 4)[:, :, 0:HALF])
-        nc.scalar.dma_start(out=kb_t[:], in_=kb.rearrange("(p j) o -> p (j o)", j=PACK))
-        nc.scalar.dma_start(out=t_t[:], in_=t.rearrange("(p j) o -> p (j o)", j=PACK))
+        for kv in range(KV):
+            lo = 2 * ROWS * kv
+            (nc.sync, nc.scalar)[kv].dma_start(out=k_raw[lo : lo + ROWS], in_=kT[kv].rearrange("(p j) n -> p j n", j=PACK))
+            nc.vector.memset(k_raw[lo + ROWS : lo + 2 * ROWS].rearrange("p j n -> p (j n)").bitcast(I32), 0)
+        mask_rows = mask.rearrange("(p r) n -> p r n", r=PACK)
+        nc.sync.dma_start(out=q_first[0][:], in_=q_rows(SETS[0][0], 4)[:, :, 0:HALF])
+        nc.scalar.dma_start(out=kb_t[:], in_=kb.rearrange("(p r) o -> p (r o)", r=PACK))
+        nc.scalar.dma_start(out=t_t[:], in_=t.rearrange("(p r) o -> p (r o)", r=PACK))
         nc.sync.dma_start(out=m_raw[0][:], in_=mask_rows[:, :, 0:HALF])
-        nc.sync.dma_start(out=q_raw[0, 1][:], in_=q_rows(2, 4)[:, :, HALF:NQ])
-        nc.sync.dma_start(out=v_raw[:].rearrange("p k j e -> p k (j e)"), in_=v.rearrange("k (p j) e -> p k (j e)", j=PACK))
-        nc.sync.dma_start(out=m_raw[1][:], in_=mask_rows[:, :, HALF:NQ])
-        nc.sync.dma_start(out=q_raw1[0:64], in_=q_rows(0, 2))
+        nc.sync.dma_start(out=q_first[1][:], in_=q_rows(SETS[0][0], 4)[:, :, HALF:NQ])
+        nc.sync.dma_start(out=v_raw[:].rearrange("p k r e -> p k (r e)"), in_=v.rearrange("k (p r) e -> p k (r e)", r=PACK))
 
-        def copy_on(eng, dst, src):
-            if eng == "v":
-                nc.vector.tensor_copy(out=dst, in_=src)
-            else:
-                nc.scalar.copy(out=dst, in_=src)
+        k_bf = [sb("k_bf%d" % pair, [P, 2, CH, PACK], BF16) for pair in range(2)]
+        k_mx = sb("k_mx", [P, N + N // PACK], I32)
+        k_codes = k_mx[:, 0:N]
+        k_scales = k_mx[:, N : N + N // PACK].bitcast(U8)
+        nc.vector.memset(k_mx[:, N : N + N // PACK], 0)
 
-        def quantize(codes, scales, vals):
-            nc.vector.quantize_mx(out=codes.bitcast(FP8X4), scales=scales, in_=vals)
+        def cast_k(pair, engine):
+            src = k_raw[:].rearrange("p j (s r) -> p s j r", r=PACK)[:, :, :, 2 * pair : 2 * pair + 2]
+            copy_on(engine, k_bf[pair][:].rearrange("p r s j -> p s j r"), src)
+
+        def quant_k(pair):
+            cols = slice(2 * CH * pair, 2 * CH * (pair + 1))
+            quantize(k_codes[:, cols], k_scales[:, cols], k_bf[pair][:].rearrange("p r s j -> p (r s j)"))
+
+        def share_k():
+            for kv in range(KV):
+                lo = 2 * ROWS * kv
+                nc.scalar.dma_start(out=k_mx[lo + ROWS : lo + 2 * ROWS], in_=k_mx[lo : lo + ROWS])
 
         q_bf, q_codes, q_scales = {}, {}, {}
 
-        def cast_q(s, c0, nchunk, eng):
-            w = nchunk * CH
-            key = (s, c0)
-            q_bf[key] = sb("q_bf%d_%d" % key, [P, w, PACK], BF16)
+        def cast_q(s, c0, chunks, engine):
+            width = chunks * CH
+            q_bf[s, c0] = sb("q_bf%d_%d" % (s, c0), [P, width, PACK], BF16)
             if s == 0:
-                src = q_raw[0, c0 // 2][:, :, (c0 % 2) * CH : (c0 % 2) * CH + w]
+                src = q_first[c0 // 2][:, :, (c0 % 2) * CH : (c0 % 2) * CH + width]
             else:
-                src = q_raw1[:, :, c0 * CH : c0 * CH + w]
-            copy_on(eng, q_bf[key][:].rearrange("p (c i) j -> p c j i", i=CAST_RUN), src.rearrange("p j (c i) -> p c j i", i=CAST_RUN))
+                src = q_second[:, :, c0 * CH : c0 * CH + width]
+            dst = q_bf[s, c0][:].rearrange("p (c i) j -> p c j i", i=RUN)
+            copy_on(engine, dst, src.rearrange("p j (c i) -> p c j i", i=RUN))
 
-        def quant_q(s, c0, nchunk):
-            w = nchunk * CH
-            key = (s, c0)
-            codes = sb("q_codes%d_%d" % key, [P, w], U32)
-            scales = sb("q_scales%d_%d" % key, [P, w], U8)
-            quantize(codes[:], scales[:], q_bf[key][:].rearrange("p n j -> p (n j)"))
-            for c in range(nchunk):
+        def quant_q(s, c0, chunks):
+            codes = sb("q_codes%d_%d" % (s, c0), [P, chunks * CH], U32)
+            scales = sb("q_scales%d_%d" % (s, c0), [P, chunks * CH], U8)
+            quantize(codes[:], scales[:], q_bf[s, c0][:].rearrange("p n j -> p (n j)"))
+            for c in range(chunks):
                 q_codes[s, c0 + c] = codes[:, c * CH : (c + 1) * CH]
                 q_scales[s, c0 + c] = scales[:, c * CH : (c + 1) * CH]
-
-        k_bf = [sb("k_bf%d" % rp, [P, 2, CH, PACK], BF16) for rp in range(2)]
-        k_codes = [sb("k_codes%d" % rp, [P, 2 * CH], U32) for rp in range(2)]
-        k_scales = [sb("k_scales%d" % rp, [P, 2 * CH], U8) for rp in range(2)]
-
-        def cast_k(rp, eng):
-            src = k_raw[:].rearrange("p j (s r) -> p s j r", r=PACK)[:, :, :, 2 * rp : 2 * rp + 2]
-            copy_on(eng, k_bf[rp][:].rearrange("p r s j -> p s j r"), src)
-
-        def quant_k(rp):
-            quantize(k_codes[rp][:], k_scales[rp][:], k_bf[rp][:].rearrange("p r s j -> p (r s j)"))
 
         v_bf = sb("v_bf", [P, KV, D, PACK], BF16)
         v_codes = sb("v_codes", [P, KV * D], U32)
         v_scales = sb("v_scales", [P, KV * D], U8)
 
-        def cast_v(eng):
-            copy_on(eng, v_bf[:].rearrange("p k (c i) j -> p k c j i", i=CAST_RUN), v_raw[:].rearrange("p k j (c i) -> p k c j i", i=CAST_RUN))
+        def cast_v():
+            dst = v_bf[:].rearrange("p k (c i) r -> p k c r i", i=RUN)
+            nc.scalar.copy(out=dst, in_=v_raw[:].rearrange("p k r (c i) -> p k c r i", i=RUN))
 
         def quant_v():
-            quantize(v_codes[:], v_scales[:], v_bf[:].rearrange("p k e j -> p (k e j)"))
+            quantize(v_codes[:], v_scales[:], v_bf[:].rearrange("p k e r -> p (k e r)"))
 
         mt = sb("mt", [P, NQ * PACK], F32)
 
         def make_mt(u):
-            half = mt[:, u * HALF * PACK : (u + 1) * HALF * PACK].rearrange("p (c r i) -> p c r i", r=PACK, i=MUL_RUN)
+            dealt = mt[:, u * HALF * PACK : (u + 1) * HALF * PACK].rearrange("p (x c r i) -> p r c i x", x=2, r=PACK, i=RUN)
             for r in range(PACK):
-                nc.vector.tensor_scalar(out=half[:, :, r, :], in0=m_raw[u][:, r, :].rearrange("p (c i) -> p c i", i=MUL_RUN), scalar1=t_t[:, r : r + 1], scalar2=1.0 / 32.0, op0=ALU.mult, op1=ALU.mult)
+                nc.vector.tensor_scalar(
+                    out=dealt[:, r],
+                    in0=m_raw[u][:, r, :].rearrange("p (c i x) -> p c i x", i=RUN, x=2),
+                    scalar1=t_t[:, r : r + 1],
+                    scalar2=1.0 / 32.0,
+                    op0=ALU.mult,
+                    op1=ALU.mult,
+                )
 
-        def half_item(g, u, rp):
-            return (0, g, (2 * rp, 2 * rp + 1), 2 * u, 2)
+        def half_item(g, u, pair):
+            return (0, g, (2 * pair, 2 * pair + 1), 2 * u, 2)
 
         def full_item(s, g, r):
-            return (s, g, (r,), 0, 4)
+            return (s, g, (r,), 0, NQ // CH)
 
         def bank_of(item):
-            s, g, rs, c0, nch = item
-            banks = score_banks[g]
-            return banks[(rs[0] // len(rs)) % len(banks)]
+            g, places = item[1], item[2]
+            return (g, (places[0] // len(places)) % len(score_banks[g]))
 
-        def fill(*items):
-            calls = [[(item, n, r, c) for c in range(item[4]) for n, r in enumerate(item[2])] for item in items]
+        def fill(items):
+            calls = [[(item, n, c) for c in range(item[4]) for n in range(len(item[2]))] for item in items]
             for group in zip(*calls):
-                for item, n, r, c in group:
-                    s, g, rs, c0, nch = item
+                for item, n, c in group:
+                    s, g, places, c0, chunks = item
                     rows = slice(ROWS * g, ROWS * (g + 1))
-                    col = (n * nch + c) * CH
-                    kc = slice((r % 2) * CH, (r % 2 + 1) * CH)
-                    nc.tensor.matmul_mx(
-                        out=bank_of(item)[:, col : col + CH],
-                        lhsT=k_codes[r // 2][rows, kc].bitcast(FP8X4),
-                        lhsT_scale=k_scales[r // 2][rows, kc],
-                        rhs=q_codes[s, c0 + c][rows].bitcast(FP8X4),
-                        rhs_scale=q_scales[s, c0 + c][rows],
-                        start=True,
-                        stop=True,
-                    )
+                    keys = slice(places[n] * CH, (places[n] + 1) * CH)
+                    col = (n * chunks + c) * CH
+                    bank = score_banks[g][bank_of(item)[1]]
+                    multiply(bank[:, col : col + CH], k_codes[rows, keys], k_scales[rows, keys], q_codes[s, c0 + c][rows], q_scales[s, c0 + c][rows])
 
         p_t = {}
 
         def tanh(item):
-            s, g, rs, c0, nch = item
-            w = nch * CH
-            key = (s, g, c0)
-            if rs[0] == 0:
-                p_t[key] = sb("p%d_%d_%d" % key, [P, PACK, w], F32)
-            for n, r in enumerate(rs):
-                nc.scalar.activation(out=p_t[key][:, r, :], in_=bank_of(item)[:, n * w : (n + 1) * w], func=ACT.Tanh, bias=kb_t[:, r : r + 1])
+            s, g, places, c0, chunks = item
+            width = chunks * CH
+            if places[0] == 0:
+                p_t[s, g, c0] = sb("p%d_%d_%d" % (s, g, c0), [P, PACK, width], F32)
+            bank = score_banks[g][bank_of(item)[1]]
+            for n, r in enumerate(places):
+                nc.scalar.activation(
+                    out=p_t[s, g, c0][:, r, :].rearrange("p (u x a) -> p u x a", x=2, a=CH),
+                    in_=bank[:, n * width : (n + 1) * width].rearrange("p (u a x) -> p u x a", x=2, a=CH),
+                    func=ACT.Tanh,
+                    bias=kb_t[:, r : r + 1],
+                )
 
-        def gate_view(s, g):
-            return gate[2 * s + g // 2][:, g % 2].rearrange("p m e -> p (m e)")
+        def gate_of(s, g):
+            return gate[2 * s + g // 2][:, g % 2, :]
 
         def gate_tanh(s, g):
-            nc.scalar.activation(out=gate_view(s, g), in_=gate_view(s, g), func=ACT.Tanh, scale=0.5)
+            nc.scalar.activation(out=gate_of(s, g), in_=gate_of(s, g), func=ACT.Tanh, scale=0.5)
 
         w_bf, w_codes, w_scales = {}, {}, {}
 
-        def weigh(s, g, c0, nch):
-            w = nch * CH
-            w_bf[s, g, c0] = work.tile([P, w, PACK], BF16, name="w_bf", align_bytes=64)
+        def weigh(s, g, c0=0, chunks=NQ // CH):
+            width = chunks * CH
+            w_bf[s, g, c0] = work.tile([P, width, PACK], BF16, name="w_bf", align_bytes=64)
             if (s, g, c0) in p_t:
-                src = p_t[s, g, c0][:, :, 0:w]
+                src = p_t[s, g, c0][:, :, 0:width]
             else:
-                src = p_t[s, g, 0][:, :, c0 * CH : c0 * CH + w]
+                src = p_t[s, g, 0][:, :, c0 * CH : c0 * CH + width]
             nc.vector.tensor_tensor(
-                out=w_bf[s, g, c0][:].rearrange("p (c i) r -> p c r i", i=MUL_RUN),
-                in0=src.rearrange("p r (c i) -> p c r i", i=MUL_RUN),
-                in1=mt[:, c0 * CH * PACK : (c0 * CH + w) * PACK].rearrange("p (c r i) -> p c r i", r=PACK, i=MUL_RUN),
+                out=w_bf[s, g, c0][:].rearrange("p (c i) r -> p c r i", i=RUN),
+                in0=src.rearrange("p r (c i) -> p c r i", i=RUN),
+                in1=mt[:, c0 * CH * PACK : (c0 * CH + width) * PACK].rearrange("p (c r i) -> p c r i", r=PACK, i=RUN),
                 op=ALU.mult,
             )
 
-        def quant_w(s, g, c0, nch):
-            w = nch * CH
-            codes = work.tile([P, w], U32, name="w_codes", align_bytes=64)
-            scales = work.tile([P, w], U8, name="w_scales", align_bytes=64)
+        def quant_w(s, g, c0=0, chunks=NQ // CH):
+            codes = work.tile([P, chunks * CH], U32, name="w_codes", align_bytes=64)
+            scales = work.tile([P, chunks * CH], U8, name="w_scales", align_bytes=64)
             quantize(codes[:], scales[:], w_bf[s, g, c0][:].rearrange("p n r -> p (n r)"))
-            for c in range(nch):
+            for c in range(chunks):
                 w_codes[s, g, c0 + c] = codes[:, c * CH : (c + 1) * CH]
                 w_scales[s, g, c0 + c] = scales[:, c * CH : (c + 1) * CH]
 
-        def values(s, g, c0=0, nch=4):
-            kv = g // 2
-            for c in range(c0, c0 + nch):
-                nc.tensor.matmul_mx(
-                    out=y_bank[:, c * CH : (c + 1) * CH],
-                    lhsT=w_codes[s, g, c].bitcast(FP8X4),
-                    lhsT_scale=w_scales[s, g, c],
-                    rhs=v_codes[:, kv * D : (kv + 1) * D].bitcast(FP8X4),
-                    rhs_scale=v_scales[:, kv * D : (kv + 1) * D],
-                    start=True,
-                    stop=True,
-                )
+        def second_product(s, g, c0=0, chunks=NQ // CH):
+            cols = slice((g // 2) * D, (g // 2 + 1) * D)
+            for c in range(c0, c0 + chunks):
+                multiply(y_bank[:, c * CH : (c + 1) * CH], w_codes[s, g, c], w_scales[s, g, c], v_codes[:, cols], v_scales[:, cols])
 
-        def finish(s, g, parts=1):
-            w = NQ // parts
-            for u in range(parts):
-                res = sb("res%d_%d_%d" % (s, g, u), [P, w], F32)
-                cols = slice(u * w, (u + 1) * w)
-                nc.vector.scalar_tensor_tensor(out=res[:], in0=gate_view(s, g)[:, cols], scalar=1.0, in1=y_bank[:, cols], op0=ALU.add, op1=ALU.mult)
-                (nc.sync, nc.scalar)[u].dma_start(out=out[SETS[s][g], cols, :].rearrange("(m p) e -> p m e", p=P), in_=res[:].rearrange("p (m e) -> p m e", e=D))
+        def finish(s, g, c0=0, chunks=NQ // CH):
+            cols = slice(c0 * CH, (c0 + chunks) * CH)
+            result = sb("result%d_%d_%d" % (s, g, c0), [P, chunks * CH], F32)
+            nc.vector.scalar_tensor_tensor(out=result[:], in0=gate_of(s, g)[:, cols], scalar=1.0, in1=y_bank[:, cols], op0=ALU.add, op1=ALU.mult)
+            rows = out[SETS[s][g]].rearrange("(u a x) e -> a u (x e)", u=2, x=2)
+            nc.sync.dma_start(out=rows[:, c0 // 2 : (c0 + chunks) // 2, :], in_=result[:].rearrange("p (u c) -> p u c", c=HALF))
 
-        A, B, C, E = 0, 1, 2, 3
-        items = [half_item(A, 0, 0), half_item(A, 0, 1), half_item(B, 0, 0), half_item(B, 0, 1), half_item(A, 1, 0), half_item(A, 1, 1)]
-        items.extend([half_item(B, 1, 0), full_item(0, C, 0), half_item(B, 1, 1), full_item(0, C, 1)])
-        items.extend([full_item(0, E, 0), full_item(0, C, 2), full_item(0, E, 1), full_item(0, C, 3)])
-        items.extend([full_item(0, E, 2), full_item(1, A, 0), full_item(0, E, 3), full_item(1, A, 1)])
-        items.extend([full_item(1, B, 0), full_item(1, A, 2), full_item(1, B, 1), full_item(1, A, 3)])
-        items.extend([full_item(1, E, 0), full_item(1, B, 2), full_item(1, E, 1), full_item(1, B, 3)])
-        items.extend([full_item(1, E, 2), full_item(1, C, 0), full_item(1, E, 3), full_item(1, C, 1)])
-        items.extend([full_item(1, C, 2), full_item(1, C, 3)])
-        fills_after = {1: [(4, 7)], 2: [(5, 6)], 3: [(8, 9)], 7: [(10, 11)], 10: [(12, 13)], 12: [(14, 15)], 14: [(16, 17)], 15: [(18, 19)], 17: [(20, 21)], 18: [(22, 23)], 22: [(24, 25)], 24: [(26, 27)], 26: [(28, 29)], 27: [(30,)], 29: [(31,)]}
-        gate_after = {11: (0, A), 13: (0, B), 15: (0, C), 21: (0, E), 23: (1, A), 25: (1, B), 27: (1, E), 30: (1, C)}
-        heads = [(0, A), (0, B), (0, C), (0, E), (1, A), (1, B), (1, E), (1, C)]
-        done_at = {13: 2, 16: 3, 21: 4, 25: 5, 28: 6, 31: 7}
+        order = [half_item(g, u, pair) for u in range(2) for g in (A, B) for pair in range(2)]
+        two_banks = [full_item(s, g, r) for s, g in ((0, C), (1, A), (1, B), (1, C)) for r in range(PACK)]
+        one_bank = [full_item(s, E, r) for s in range(2) for r in range(PACK)]
+        for n, item in enumerate(one_bank):
+            order.extend([item] + two_banks[2 * n : 2 * n + 2])
+        heads = [(0, A), (0, B)] + [item[:2] for item in order if item[2] == (PACK - 1,)]
+        banks = [bank_of(item) for item in order]
+        last = len(order) - 1
+        filled = [0, 1, 2, 3]
 
-        cast_k(0, "v")
-        cast_k(1, "s")
+        def fill_ahead(j):
+            ahead = range(j + 1, min(j + LOOKAHEAD, last) + 1)
+            group = [n for n in ahead if n not in filled and banks[n] not in banks[j + 1 : n]]
+            if group:
+                fill([order[n] for n in group])
+                filled.extend(group)
+
+        cast_k(0, nc.vector)
+        cast_k(1, nc.scalar)
         quant_k(0)
-        cast_q(0, 0, 1, "v")
-        cast_q(0, 1, 1, "s")
+        cast_q(0, 0, 1, nc.vector)
+        cast_q(0, 1, 1, nc.scalar)
         quant_k(1)
         quant_q(0, 0, 1)
         quant_q(0, 1, 1)
-        fill(items[0], items[2])
-        fill(items[1], items[3])
+        share_k()
+        nc.sync.dma_start(out=m_raw[1][:], in_=mask_rows[:, :, HALF:NQ])
+        nc.sync.dma_start(out=q_second[0 : P // 2], in_=q_rows(SETS[1][0], 2))
+        fill([order[0], order[2]])
+        fill([order[1], order[3]])
         make_mt(0)
-        cast_q(0, 2, 2, "v")
-        for j, item in enumerate(items):
+        cast_q(0, 2, 2, nc.vector)
+        quant_q(0, 2, 2)
+
+        for j, item in enumerate(order):
             tanh(item)
-            if j == 1:
+            if item == half_item(A, 0, 1):
                 weigh(0, A, 0, 2)
-                quant_q(0, 2, 2)
-            if j == 2:
-                nc.scalar.dma_start(out=q_raw1[64:128], in_=q_rows(6, 2))
-                for i in range(4):
-                    load_og(i)
-            if j == 3:
-                cast_v("s")
+                nc.scalar.dma_start(out=q_second[P // 2 : P], in_=q_rows(SETS[1][2], 2))
+                for n in range(H // 2):
+                    load_og(n)
+            if item == half_item(B, 0, 1):
+                cast_v()
                 weigh(0, B, 0, 2)
                 quant_w(0, A, 0, 2)
                 make_mt(1)
                 quant_w(0, B, 0, 2)
-            if j == 5:
+            if item == half_item(A, 1, 1):
                 weigh(0, A, 2, 2)
                 quant_v()
                 quant_w(0, A, 2, 2)
-                cast_q(1, 0, 4, "v")
-            if j == 8:
+            if item == half_item(B, 1, 1):
                 weigh(0, B, 2, 2)
-                quant_q(1, 0, 4)
+                cast_q(1, 0, NQ // CH, nc.vector)
                 quant_w(0, B, 2, 2)
-            for group in fills_after.get(j, []):
-                fill(*[items[n] for n in group])
-            if j == 10:
-                values(0, A)
-            if j in gate_after:
-                gate_tanh(*gate_after[j])
-            if j == 11:
+                quant_q(1, 0, NQ // CH)
+            fill_ahead(j)
+            if item == full_item(0, C, 1):
+                gate_tanh(0, A)
+                second_product(0, A)
                 finish(0, A)
-            if j in done_at:
-                n = done_at[j]
-                s, g = heads[n]
-                values(*heads[n - 1])
-                if n < 7:
-                    weigh(s, g, 0, 4)
-                    finish(*heads[n - 1])
-                    quant_w(s, g, 0, 4)
-                else:
-                    weigh(s, g, 0, 2)
-                    weigh(s, g, 2, 2)
-                    quant_w(s, g, 0, 2)
-                    finish(*heads[n - 1])
-                    values(s, g, 0, 2)
-                    quant_w(s, g, 2, 2)
-                    values(s, g, 2, 2)
-                    finish(s, g, 2)
+            n, rest = divmod(j - 5, PACK)
+            if rest == 0 and 2 <= n < H - 1:
+                gate_tanh(*heads[n - 1])
+                second_product(*heads[n - 1])
+                weigh(*heads[n])
+                finish(*heads[n - 1])
+                quant_w(*heads[n])
+
+        gate_tanh(*heads[-2])
+        gate_tanh(*heads[-1])
+        second_product(*heads[-2])
+        weigh(*heads[-1], 0, 2)
+        finish(*heads[-2])
+        quant_w(*heads[-1], 0, 2)
+        second_product(*heads[-1], 0, 2)
+        weigh(*heads[-1], 2, 2)
+        finish(*heads[-1], 0, 2)
+        quant_w(*heads[-1], 2, 2)
+        second_product(*heads[-1], 2, 2)
+        finish(*heads[-1], 2, 2)

from contextlib import ExitStack

import concourse.mybir as mybir

H, KV, D, NQ, N = 8, 2, 128, 512, 512
FLOPS = 2 * 2 * H * N * NQ * D

F32 = mybir.dt.float32
BF16 = mybir.dt.bfloat16
I32 = mybir.dt.int32
U32 = mybir.dt.uint32
U8 = mybir.dt.uint8
FP8X4 = mybir.dt.float8_e4m3fn_x4
ALU = mybir.AluOpType
ACT = mybir.ActivationFunctionType

P = 128
PACK = 4
ROWS = 32
CH = 128
HALF = 256
RUN = 4
SETS = ((2, 3, 4, 5), (0, 1, 6, 7))
A, B, C, E = 0, 2, 1, 3
LOOKAHEAD = 4
W_BUFS = 5


def tile_rows_a_tanh_kb_mask_gate_kernel(tc, qT, kT, t, v, kb, mask, og, out):
    nc = tc.nc
    with ExitStack() as ctx:
        keep = ctx.enter_context(tc.tile_pool(name="keep", bufs=1))
        work = ctx.enter_context(tc.tile_pool(name="work", bufs=W_BUFS))
        psum = ctx.enter_context(tc.psum_pool(name="psum", bufs=1))
        ctx.enter_context(tc.manual_schedule())

        def sb(name, shape, dtype):
            return keep.tile(shape, dtype, name=name, align_bytes=64)

        def copy_on(engine, dst, src):
            if engine is nc.vector:
                nc.vector.tensor_copy(out=dst, in_=src)
            else:
                nc.scalar.copy(out=dst, in_=src)

        def quantize(codes, scales, values):
            nc.vector.quantize_mx(out=codes.bitcast(FP8X4), scales=scales, in_=values)

        def multiply(dst, lhs_codes, lhs_scales, rhs_codes, rhs_scales):
            nc.tensor.matmul_mx(
                out=dst,
                lhsT=lhs_codes.bitcast(FP8X4),
                lhsT_scale=lhs_scales,
                rhs=rhs_codes.bitcast(FP8X4),
                rhs_scale=rhs_scales,
                start=True,
                stop=True,
            )

        score_banks = [[psum.tile([P, NQ], F32, name="scores%d_%d" % (g, b)) for b in range(1 if g == E else 2)] for g in range(4)]
        y_bank = psum.tile([P, NQ], F32, name="y_bank")

        k_raw = sb("k_raw", [P, PACK, N], F32)
        kb_t = sb("kb_t", [P, PACK], F32)
        t_t = sb("t_t", [P, PACK], F32)
        q_first = [sb("q_first%d" % u, [P, PACK, HALF], F32) for u in range(2)]
        q_second = sb("q_second", [P, PACK, NQ], F32)
        m_raw = [sb("m_raw%d" % u, [P, PACK, HALF], F32) for u in range(2)]
        v_raw = sb("v_raw", [P, KV, PACK, D], F32)
        gate = [sb("gate%d" % n, [P, 2, NQ], F32) for n in range(H // 2)]

        def q_rows(h0, heads):
            return qT[h0 : h0 + heads].rearrange("h (p j) n -> (h p) j n", j=PACK)

        def load_og(n):
            h0 = SETS[n // 2][2 * (n % 2)]
            rows = og[h0 : h0 + 2].rearrange("h (u a x) e -> a (h u) (x e)", u=2, x=2)
            nc.sync.dma_start(out=gate[n][:].rearrange("p h (u c) -> p (h u) c", u=2), in_=rows)

        for kv in range(KV):
            lo = 2 * ROWS * kv
            (nc.sync, nc.scalar)[kv].dma_start(out=k_raw[lo : lo + ROWS], in_=kT[kv].rearrange("(p j) n -> p j n", j=PACK))
            nc.vector.memset(k_raw[lo + ROWS : lo + 2 * ROWS].rearrange("p j n -> p (j n)").bitcast(I32), 0)
        mask_rows = mask.rearrange("(p r) n -> p r n", r=PACK)
        nc.sync.dma_start(out=q_first[0][:], in_=q_rows(SETS[0][0], 4)[:, :, 0:HALF])
        nc.scalar.dma_start(out=kb_t[:], in_=kb.rearrange("(p r) o -> p (r o)", r=PACK))
        nc.scalar.dma_start(out=t_t[:], in_=t.rearrange("(p r) o -> p (r o)", r=PACK))
        nc.sync.dma_start(out=m_raw[0][:], in_=mask_rows[:, :, 0:HALF])
        nc.sync.dma_start(out=q_first[1][:], in_=q_rows(SETS[0][0], 4)[:, :, HALF:NQ])
        nc.sync.dma_start(out=v_raw[:].rearrange("p k r e -> p k (r e)"), in_=v.rearrange("k (p r) e -> p k (r e)", r=PACK))

        k_bf = [sb("k_bf%d" % pair, [P, 2, CH, PACK], BF16) for pair in range(2)]
        k_mx = sb("k_mx", [P, N + N // PACK], I32)
        k_codes = k_mx[:, 0:N]
        k_scales = k_mx[:, N : N + N // PACK].bitcast(U8)
        nc.vector.memset(k_mx[:, N : N + N // PACK], 0)

        def cast_k(pair, engine):
            src = k_raw[:].rearrange("p j (s r) -> p s j r", r=PACK)[:, :, :, 2 * pair : 2 * pair + 2]
            copy_on(engine, k_bf[pair][:].rearrange("p r s j -> p s j r"), src)

        def quant_k(pair):
            cols = slice(2 * CH * pair, 2 * CH * (pair + 1))
            quantize(k_codes[:, cols], k_scales[:, cols], k_bf[pair][:].rearrange("p r s j -> p (r s j)"))

        def share_k():
            for kv in range(KV):
                lo = 2 * ROWS * kv
                nc.scalar.dma_start(out=k_mx[lo + ROWS : lo + 2 * ROWS], in_=k_mx[lo : lo + ROWS])

        q_bf, q_codes, q_scales = {}, {}, {}

        def cast_q(s, c0, chunks, engine):
            width = chunks * CH
            q_bf[s, c0] = sb("q_bf%d_%d" % (s, c0), [P, width, PACK], BF16)
            if s == 0:
                src = q_first[c0 // 2][:, :, (c0 % 2) * CH : (c0 % 2) * CH + width]
            else:
                src = q_second[:, :, c0 * CH : c0 * CH + width]
            dst = q_bf[s, c0][:].rearrange("p (c i) j -> p c j i", i=RUN)
            copy_on(engine, dst, src.rearrange("p j (c i) -> p c j i", i=RUN))

        def quant_q(s, c0, chunks):
            codes = sb("q_codes%d_%d" % (s, c0), [P, chunks * CH], U32)
            scales = sb("q_scales%d_%d" % (s, c0), [P, chunks * CH], U8)
            quantize(codes[:], scales[:], q_bf[s, c0][:].rearrange("p n j -> p (n j)"))
            for c in range(chunks):
                q_codes[s, c0 + c] = codes[:, c * CH : (c + 1) * CH]
                q_scales[s, c0 + c] = scales[:, c * CH : (c + 1) * CH]

        v_bf = sb("v_bf", [P, KV, D, PACK], BF16)
        v_codes = sb("v_codes", [P, KV * D], U32)
        v_scales = sb("v_scales", [P, KV * D], U8)

        def cast_v():
            dst = v_bf[:].rearrange("p k (c i) r -> p k c r i", i=RUN)
            nc.scalar.copy(out=dst, in_=v_raw[:].rearrange("p k r (c i) -> p k c r i", i=RUN))

        def quant_v():
            quantize(v_codes[:], v_scales[:], v_bf[:].rearrange("p k e r -> p (k e r)"))

        mt = sb("mt", [P, NQ * PACK], F32)

        def make_mt(u):
            dealt = mt[:, u * HALF * PACK : (u + 1) * HALF * PACK].rearrange("p (x c r i) -> p r c i x", x=2, r=PACK, i=RUN)
            for r in range(PACK):
                nc.vector.tensor_scalar(
                    out=dealt[:, r],
                    in0=m_raw[u][:, r, :].rearrange("p (c i x) -> p c i x", i=RUN, x=2),
                    scalar1=t_t[:, r : r + 1],
                    scalar2=1.0 / 32.0,
                    op0=ALU.mult,
                    op1=ALU.mult,
                )

        def half_item(g, u, pair):
            return (0, g, (2 * pair, 2 * pair + 1), 2 * u, 2)

        def full_item(s, g, r):
            return (s, g, (r,), 0, NQ // CH)

        def bank_of(item):
            g, places = item[1], item[2]
            return (g, (places[0] // len(places)) % len(score_banks[g]))

        def fill(items):
            calls = [[(item, n, c) for c in range(item[4]) for n in range(len(item[2]))] for item in items]
            for group in zip(*calls):
                for item, n, c in group:
                    s, g, places, c0, chunks = item
                    rows = slice(ROWS * g, ROWS * (g + 1))
                    keys = slice(places[n] * CH, (places[n] + 1) * CH)
                    col = (n * chunks + c) * CH
                    bank = score_banks[g][bank_of(item)[1]]
                    multiply(bank[:, col : col + CH], k_codes[rows, keys], k_scales[rows, keys], q_codes[s, c0 + c][rows], q_scales[s, c0 + c][rows])

        p_t = {}

        def tanh(item):
            s, g, places, c0, chunks = item
            width = chunks * CH
            if places[0] == 0:
                p_t[s, g, c0] = sb("p%d_%d_%d" % (s, g, c0), [P, PACK, width], F32)
            bank = score_banks[g][bank_of(item)[1]]
            for n, r in enumerate(places):
                nc.scalar.activation(
                    out=p_t[s, g, c0][:, r, :].rearrange("p (u x a) -> p u x a", x=2, a=CH),
                    in_=bank[:, n * width : (n + 1) * width].rearrange("p (u a x) -> p u x a", x=2, a=CH),
                    func=ACT.Tanh,
                    bias=kb_t[:, r : r + 1],
                )

        def gate_of(s, g):
            return gate[2 * s + g // 2][:, g % 2, :]

        def gate_tanh(s, g):
            nc.scalar.activation(out=gate_of(s, g), in_=gate_of(s, g), func=ACT.Tanh, scale=0.5)

        w_bf, w_codes, w_scales = {}, {}, {}

        def weigh(s, g, c0=0, chunks=NQ // CH):
            width = chunks * CH
            w_bf[s, g, c0] = work.tile([P, width, PACK], BF16, name="w_bf", align_bytes=64)
            if (s, g, c0) in p_t:
                src = p_t[s, g, c0][:, :, 0:width]
            else:
                src = p_t[s, g, 0][:, :, c0 * CH : c0 * CH + width]
            nc.vector.tensor_tensor(
                out=w_bf[s, g, c0][:].rearrange("p (c i) r -> p c r i", i=RUN),
                in0=src.rearrange("p r (c i) -> p c r i", i=RUN),
                in1=mt[:, c0 * CH * PACK : (c0 * CH + width) * PACK].rearrange("p (c r i) -> p c r i", r=PACK, i=RUN),
                op=ALU.mult,
            )

        def quant_w(s, g, c0=0, chunks=NQ // CH):
            codes = work.tile([P, chunks * CH], U32, name="w_codes", align_bytes=64)
            scales = work.tile([P, chunks * CH], U8, name="w_scales", align_bytes=64)
            quantize(codes[:], scales[:], w_bf[s, g, c0][:].rearrange("p n r -> p (n r)"))
            for c in range(chunks):
                w_codes[s, g, c0 + c] = codes[:, c * CH : (c + 1) * CH]
                w_scales[s, g, c0 + c] = scales[:, c * CH : (c + 1) * CH]

        def second_product(s, g, c0=0, chunks=NQ // CH):
            cols = slice((g // 2) * D, (g // 2 + 1) * D)
            for c in range(c0, c0 + chunks):
                multiply(y_bank[:, c * CH : (c + 1) * CH], w_codes[s, g, c], w_scales[s, g, c], v_codes[:, cols], v_scales[:, cols])

        def finish(s, g, c0=0, chunks=NQ // CH):
            cols = slice(c0 * CH, (c0 + chunks) * CH)
            result = sb("result%d_%d_%d" % (s, g, c0), [P, chunks * CH], F32)
            nc.vector.scalar_tensor_tensor(out=result[:], in0=gate_of(s, g)[:, cols], scalar=1.0, in1=y_bank[:, cols], op0=ALU.add, op1=ALU.mult)
            rows = out[SETS[s][g]].rearrange("(u a x) e -> a u (x e)", u=2, x=2)
            nc.sync.dma_start(out=rows[:, c0 // 2 : (c0 + chunks) // 2, :], in_=result[:].rearrange("p (u c) -> p u c", c=HALF))

        order = [half_item(g, u, pair) for u in range(2) for g in (A, B) for pair in range(2)]
        two_banks = [full_item(s, g, r) for s, g in ((0, C), (1, A), (1, B), (1, C)) for r in range(PACK)]
        one_bank = [full_item(s, E, r) for s in range(2) for r in range(PACK)]
        for n, item in enumerate(one_bank):
            order.extend([item] + two_banks[2 * n : 2 * n + 2])
        heads = [(0, A), (0, B)] + [item[:2] for item in order if item[2] == (PACK - 1,)]
        banks = [bank_of(item) for item in order]
        last = len(order) - 1
        filled = [0, 1, 2, 3]

        def fill_ahead(j):
            ahead = range(j + 1, min(j + LOOKAHEAD, last) + 1)
            group = [n for n in ahead if n not in filled and banks[n] not in banks[j + 1 : n]]
            if group:
                fill([order[n] for n in group])
                filled.extend(group)

        cast_k(0, nc.vector)
        cast_k(1, nc.scalar)
        quant_k(0)
        cast_q(0, 0, 1, nc.vector)
        cast_q(0, 1, 1, nc.scalar)
        quant_k(1)
        quant_q(0, 0, 1)
        quant_q(0, 1, 1)
        share_k()
        nc.sync.dma_start(out=m_raw[1][:], in_=mask_rows[:, :, HALF:NQ])
        nc.sync.dma_start(out=q_second[0 : P // 2], in_=q_rows(SETS[1][0], 2))
        fill([order[0], order[2]])
        fill([order[1], order[3]])
        make_mt(0)
        cast_q(0, 2, 2, nc.vector)
        quant_q(0, 2, 2)

        for j, item in enumerate(order):
            tanh(item)
            if item == half_item(A, 0, 1):
                weigh(0, A, 0, 2)
                nc.scalar.dma_start(out=q_second[P // 2 : P], in_=q_rows(SETS[1][2], 2))
                for n in range(H // 2):
                    load_og(n)
            if item == half_item(B, 0, 1):
                cast_v()
                weigh(0, B, 0, 2)
                quant_w(0, A, 0, 2)
                make_mt(1)
                quant_w(0, B, 0, 2)
            if item == half_item(A, 1, 1):
                weigh(0, A, 2, 2)
                quant_v()
                quant_w(0, A, 2, 2)
            if item == half_item(B, 1, 1):
                weigh(0, B, 2, 2)
                cast_q(1, 0, NQ // CH, nc.vector)
                quant_w(0, B, 2, 2)
                quant_q(1, 0, NQ // CH)
            fill_ahead(j)
            if item == full_item(0, C, 1):
                gate_tanh(0, A)
                second_product(0, A)
                finish(0, A)
            n, rest = divmod(j - 5, PACK)
            if rest == 0 and 2 <= n < H - 1:
                gate_tanh(*heads[n - 1])
                second_product(*heads[n - 1])
                weigh(*heads[n])
                finish(*heads[n - 1])
                quant_w(*heads[n])

        gate_tanh(*heads[-2])
        gate_tanh(*heads[-1])
        second_product(*heads[-2])
        weigh(*heads[-1], 0, 2)
        finish(*heads[-2])
        quant_w(*heads[-1], 0, 2)
        second_product(*heads[-1], 0, 2)
        weigh(*heads[-1], 2, 2)
        finish(*heads[-1], 0, 2)
        quant_w(*heads[-1], 2, 2)
        second_product(*heads[-1], 2, 2)
        finish(*heads[-1], 2, 2)
